import numpy as np
import ml_dtypes


def mxq(x, axis, fmt="e4m3"):
    dtype, down = {"e4m3": (ml_dtypes.float8_e4m3fn, 7), "e5m2": (ml_dtypes.float8_e5m2, 14)}[fmt]
    v = np.moveaxis(np.asarray(x, np.float32).astype(ml_dtypes.bfloat16).astype(np.float64), axis, -1)
    blocks = v.reshape(v.shape[:-1] + (-1, 32))
    amax = np.abs(blocks).max(-1, keepdims=True)
    byte = np.maximum(np.where(amax > 0, np.frexp(amax)[1] - 1 + 127, 0) - down, 1)
    scale = np.exp2(byte - 127.0)
    codes = (blocks / scale).astype(np.float32).astype(dtype).astype(np.float64)
    return np.moveaxis((codes * scale).reshape(v.shape), -1, axis)


WIDE = False


def mx_kscale(k):
    if not WIDE:
        return np.ones(k)
    levels = np.array([10, -10, 5, -5, 0])
    if k % 512:
        return np.exp2(np.random.permutation(np.resize(levels, k // 32))).repeat(32)
    a = np.empty((k // 512, 16))
    for p in range(k // 512):
        a[p, :8] = np.random.permutation(np.resize(levels, 8))
        for g in range(8):
            far = levels[np.abs(levels - a[p, g]) >= 10]
            a[p, g + 8] = far[np.random.randint(len(far))]
    return np.exp2(a.ravel()).repeat(32)


BF16 = ml_dtypes.bfloat16


def bf(x):
    return np.asarray(x, np.float32).astype(BF16)


def f64(x):
    return np.asarray(x).astype(np.float64)


E2M1 = np.array([0.0, 0.5, 1.0, 1.5, 2.0, 3.0, 4.0, 6.0, -0.0, -0.5, -1.0, -1.5, -2.0, -3.0, -4.0, -6.0])


def pack_weight(w, fmt):
    k, n = w.shape
    w = f64(bf(w)).reshape(k // 32, 32, n)
    amax = np.abs(w).max(1)
    if fmt == "e4m3":
        byte = np.frexp(amax)[1] - 1 + 127 - 7
    else:
        mant, ex = np.frexp(amax / 6.0)
        byte = np.where(mant > 0.5, ex, ex - 1) + 127
    byte = np.clip(np.where(amax > 0, byte, 1), 1, 254)
    scaled = (w * np.exp2(127.0 - byte)[:, None, :]).reshape(k, n).astype(np.float32)
    by_word = np.ascontiguousarray(scaled.reshape(k // 512, 128, 4, n).transpose(0, 1, 3, 2))
    if fmt == "e4m3":
        words = by_word.astype(ml_dtypes.float8_e4m3fn).view(np.uint8)
    else:
        c = by_word.astype(ml_dtypes.float4_e2m1fn).view(np.uint8) & 0xF
        words = c[..., 0::2] | (c[..., 1::2] << 4)
    return np.ascontiguousarray(words), np.ascontiguousarray(byte.astype(np.uint8).reshape(k // 512, 16, n))


def unpack_weight(words, scales, fmt):
    g, p, n, _ = words.shape
    if fmt == "e4m3":
        vals = np.ascontiguousarray(words).view(ml_dtypes.float8_e4m3fn).astype(np.float64)
    else:
        nib = np.empty((g, p, n, 4), np.uint8)
        nib[..., 0::2] = words & 0xF
        nib[..., 1::2] = words >> 4
        vals = E2M1[nib]
    vals = vals * np.repeat(np.exp2(scales.astype(np.float64) - 127.0), 8, axis=1)[..., None]
    return vals.transpose(0, 1, 3, 2).reshape(g * 512, n)
def pack4(w):
    words, scales = pack_weight(w, "e2m1")
    return words.reshape(words.shape[0], 128, -1), scales


def unpack4(words, scales):
    return unpack_weight(words.reshape(words.shape[0], 128, -1, 2), scales, "e2m1")


T, D, E = 2048, 1024, 512


def setup_inputs():
    s = mx_kscale(D)
    z = np.random.standard_normal((T, D)) * np.exp(0.3 * np.random.standard_normal((T, 1)))
    inv_len = 1.0 / np.sqrt(np.sum(z * z, axis=1))
    a = np.random.standard_normal((D, E))
    b = np.random.standard_normal((D, E))
    c = np.random.standard_normal((D, E))
    a = a / np.sqrt(np.sum(a * a, axis=0))
    b = b / np.sqrt(np.sum(b * b, axis=0))
    c = c / np.sqrt(np.sum(c * c, axis=0))
    a_words, a_scales = pack4(a / s[:, None])
    b_words, b_scales = pack_weight(b / s[:, None], "e4m3")
    return {"z": bf(z * s),
            "a_words": a_words, "a_scales": a_scales,
            "b_words": b_words, "b_scales": b_scales,
            "c": bf(c / s[:, None]),
            "inv_len": bf(inv_len),
            "tau": bf(np.sqrt(D) * (1 + 0.1 * np.random.standard_normal(E)))}


def reference(z, a_words, a_scales, b_words, b_scales, c, inv_len, tau):
    zq = mxq(f64(z), 1, "e4m3")
    old = zq @ unpack4(a_words, a_scales)
    mid = zq @ unpack_weight(b_words, b_scales, "e4m3")
    new = zq @ mxq(f64(c), 0, "e4m3")
    best = np.maximum(np.maximum(old, mid), new)
    return best * f64(inv_len)[:, None] * f64(tau)

@@ -1,0 +1,320 @@
+from contextlib import ExitStack
+
+import concourse.mybir as mybir
+from concourse.masks import make_identity
+
+T, D, E = 2048, 1024, 512
+P = 128
+NT = T // P
+G = 2
+FLOPS = 3 * 2 * T * D * E
+
+F32 = mybir.dt.float32
+BF16 = mybir.dt.bfloat16
+I32 = mybir.dt.int32
+U32 = mybir.dt.uint32
+U8 = mybir.dt.uint8
+FP8X4 = mybir.dt.float8_e4m3fn_x4
+FP4X4 = mybir.dt.float4_e2m1fn_x4
+OP = mybir.AluOpType
+
+DIRECT = 6
+CV = 384
+POOL_F = (0, 1, 2, 3, 12, 13)
+
+
+def tile_cosine_prototype_router_s10_kernel(
+    tc, z, a_words, a_scales, b_words, b_scales, c, inv_len, tau, out
+):
+    nc = tc.nc
+    z_view = z.rearrange("(p i) d -> p i d", i=NT)
+    out_view = out.rearrange("(p i) e -> p i e", i=NT)
+
+    with ExitStack() as ctx:
+        keep = ctx.enter_context(tc.tile_pool(name="keep", bufs=1))
+        work = ctx.enter_context(tc.tile_pool(name="work", bufs=6))
+        psum = ctx.enter_context(tc.psum_pool(name="psum", bufs=2))
+        ctx.enter_context(tc.manual_schedule())
+
+        a_sb = keep.tile([P, G, 2 * E], U8, name="a_sb", align_bytes=64)
+        b_sb = keep.tile([P, G, 4 * E], U8, name="b_sb", align_bytes=64)
+        a_sc = keep.tile([P, G, E], U8, name="a_sc", align_bytes=64)
+        b_sc = keep.tile([P, G, E], U8, name="b_sc", align_bytes=64)
+        c_raw = [keep.tile([P, 4, E], BF16, name=f"c_raw{g}") for g in range(G)]
+        c_grp = [keep.tile([P, E, 4], BF16, name=f"c_grp{g}", align_bytes=64) for g in range(G)]
+        c_codes = keep.tile([P, G, E], U32, name="c_codes", align_bytes=64)
+        c_sc = keep.tile([P, G, E], U8, name="c_sc", align_bytes=64)
+        tau_raw = keep.tile([P, 4], BF16, name="tau_raw")
+        inv_raw = keep.tile([P, NT], BF16, name="inv_raw")
+        rows = {}
+
+        def load_z(i, n):
+            zt = keep.tile([P, n, D], BF16, name=f"z{i}", align_bytes=64)
+            nc.sync.dma_start(out=zt[:], in_=z_view[:, i : i + n, :])
+            for k in range(n):
+                rows[i + k] = zt[:, k, :].bitcast(F32)
+
+        def load_c(g):
+            nc.sync.dma_start(
+                out=c_raw[g][:],
+                in_=c[512 * g : 512 * (g + 1), :].rearrange("(p j) e -> p j e", j=4),
+            )
+
+        def load_scales(queue, tile, src):
+            for q in range(4):
+                queue.dma_start(
+                    out=tile[32 * q : 32 * q + 4].bitcast(I32),
+                    in_=src[:, 4 * q : 4 * q + 4, :].rearrange("g r n -> r g n").bitcast(I32),
+                )
+
+        load_z(0, 1)
+        nc.vector.memset(a_sc[:].bitcast(I32), 0)
+        nc.vector.memset(b_sc[:].bitcast(I32), 0)
+        load_scales(nc.scalar, a_sc, a_scales)
+        nc.sync.dma_start(out=a_sb[:], in_=a_words.rearrange("g p b -> p g b"))
+        load_z(1, 1)
+        nc.sync.dma_start(out=b_sb[:], in_=b_words.rearrange("g p n t -> p g (n t)"))
+        load_z(2, 2)
+        load_c(0)
+        nc.sync.dma_start(out=tau_raw[:], in_=tau.rearrange("(q j) -> q j", j=4))
+        nc.sync.dma_start(out=inv_raw[:], in_=inv_len.rearrange("(p i) -> p i", i=NT))
+        load_c(1)
+        for i in range(4, NT, 2):
+            load_z(i, 2)
+
+        ident = keep.tile([P, P], F32, name="ident")
+        make_identity(nc, ident[:])
+        load_scales(nc.gpsimd, b_sc, b_scales)
+
+        warm = keep.tile([P, 1], F32, name="warm")
+        nc.vector.memset(warm[:], 0.0)
+        nc.scalar.copy(out=warm[:], in_=warm[:])
+
+        tau_col = keep.tile([P, 4], F32, name="tau_col")
+        tau_all = keep.tile([P, P, 4], F32, name="tau_all")
+        inv = keep.tile([P, NT], F32, name="inv")
+
+        apart, bank, grouped, codes, scales = {}, {}, {}, {}, {}
+        old, mid, new, s_old, m1, m2, res = {}, {}, {}, {}, {}, {}, {}
+
+        def part(i):
+            apart[i] = work.tile([P, G, 2, P], F32, name="apart")
+            nc.scalar.copy(
+                out=apart[i][:], in_=rows[i].rearrange("p (g w u) -> p g u w", g=G, u=2)
+            )
+
+        def turn(i, halves=(0, 1), tag="xt"):
+            b = psum.tile([P, len(halves), 2, P], F32, name="xt", tag=tag)
+            for n, g in enumerate(halves):
+                for u in range(2):
+                    if i < DIRECT:
+                        src = rows[i][:, 256 * g + u : 256 * (g + 1) : 2]
+                    else:
+                        src = apart[i][:, g, u, :]
+                    nc.tensor.transpose(b[:, n, u, :], src, ident[:])
+                bank[i, g] = b[:, n]
+            bank[i] = b
+
+        def gather(i, halves=(0, 1)):
+            if i not in grouped:
+                grouped[i] = work.tile([P, G, P, 4], BF16, name="grouped", align_bytes=64)
+            lo, hi = halves[0], halves[-1] + 1
+            dst = grouped[i][:, lo:hi].rearrange("p g r t -> p (g r t)").bitcast(F32)
+            nc.scalar.copy(
+                out=dst.rearrange("p (g r u) -> p g r u", r=P, u=2),
+                in_=bank[i][:].rearrange("p g u r -> p g r u"),
+            )
+
+        def quant(i, halves=(0, 1)):
+            if i not in codes:
+                codes[i] = work.tile([P, G, P], U32, name="codes", align_bytes=64)
+                scales[i] = work.tile([P, G, P], U8, name="scales", align_bytes=64)
+            lo, hi = halves[0], halves[-1] + 1
+            nc.vector.quantize_mx(
+                out=codes[i][:, lo:hi].rearrange("p g r -> p (g r)").bitcast(FP8X4),
+                scales=scales[i][:, lo:hi].rearrange("p g r -> p (g r)"),
+                in_=grouped[i][:, lo:hi].rearrange("p g r t -> p (g r t)"),
+            )
+
+        def product(i, which, cols=(0, E), tag=None):
+            n0, n1 = cols
+            b = psum.tile([P, n1 - n0], F32, name=which, tag=tag or which)
+            for g in range(G):
+                if which == "old":
+                    rhs, sc = a_sb[:, g, 2 * n0 : 2 * n1].bitcast(FP4X4), a_sc[:, g, n0:n1]
+                elif which == "mid":
+                    rhs, sc = b_sb[:, g, 4 * n0 : 4 * n1].bitcast(FP8X4), b_sc[:, g, n0:n1]
+                else:
+                    rhs, sc = c_codes[:, g, n0:n1].bitcast(FP8X4), c_sc[:, g, n0:n1]
+                nc.tensor.matmul_mx(
+                    out=b[:],
+                    lhsT=codes[i][:, g, :].bitcast(FP8X4),
+                    lhsT_scale=scales[i][:, g, :],
+                    rhs=rhs,
+                    rhs_scale=sc,
+                    start=(g == 0),
+                    stop=(g == G - 1),
+                )
+            {"old": old, "mid": mid, "new": new}[which][i, n0] = b
+
+        def save_old(i):
+            s_old[i] = work.tile([P, E], F32, name="s_old")
+            nc.scalar.copy(out=s_old[i][:], in_=old[i, 0][:])
+
+        def max1(i, cols=(0, E)):
+            if i not in m1:
+                m1[i] = work.tile([P, E], F32, name="m1")
+            s = slice(cols[0], cols[1])
+            nc.vector.tensor_tensor(
+                out=m1[i][:, s], in0=mid[i, cols[0]][:], in1=s_old[i][:, s], op=OP.max
+            )
+
+        def max2(i, cols=(0, E)):
+            if i not in m2:
+                m2[i] = work.tile([P, E], F32, name="m2")
+            s = slice(cols[0], cols[1])
+            nc.vector.tensor_tensor(
+                out=m2[i][:, s], in0=new[i, cols[0]][:], in1=m1[i][:, s], op=OP.max
+            )
+
+        tau_flat = tau_all[:].rearrange("p q j -> p (q j)")
+
+        def finish(i, cols=(0, E)):
+            if i not in res:
+                res[i] = work.tile([P, E], F32, name="res")
+            s = slice(cols[0], cols[1])
+            if i in POOL_F:
+                nc.gpsimd.tensor_scalar(
+                    out=m2[i][:, s], in0=m2[i][:, s], scalar1=inv[:, i : i + 1], scalar2=0.0,
+                    op0=OP.mult, op1=OP.add,
+                )
+                nc.gpsimd.tensor_tensor(
+                    out=res[i][:, s], in0=m2[i][:, s], in1=tau_flat[:, s], op=OP.mult
+                )
+            else:
+                nc.vector.scalar_tensor_tensor(
+                    out=res[i][:, s], in0=m2[i][:, s], scalar=inv[:, i : i + 1],
+                    in1=tau_flat[:, s], op0=OP.mult, op1=OP.mult,
+                )
+            nc.sync.dma_start(out=out_view[:, i, s], in_=res[i][:, s])
+
+        def spread_c(engine_copy, g, lo, hi):
+            engine_copy(
+                out=c_grp[g][:, lo:hi, :], in_=c_raw[g][:, :, lo:hi].rearrange("p j e -> p e j")
+            )
+
+        def quant_c(g):
+            nc.vector.quantize_mx(
+                out=c_codes[:, g, :].bitcast(FP8X4),
+                scales=c_sc[:, g, :],
+                in_=c_grp[g][:].rearrange("p e j -> p (e j)"),
+            )
+
+        turn(0, (0,), "xt")
+        gather(0, (0,))
+        quant(0, (0,))
+        turn(0, (1,), "new")
+        gather(0, (1,))
+        quant(0, (1,))
+        turn(1)
+        gather(1)
+        quant(1)
+        product(0, "old")
+        save_old(0)
+        product(1, "old")
+        spread_c(nc.scalar.copy, 0, CV, E)
+        spread_c(nc.vector.tensor_copy, 0, 0, CV)
+        turn(2)
+        save_old(1)
+        gather(2)
+        turn(3)
+        product(0, "mid")
+        quant(2)
+        gather(3)
+        quant(3)
+        max1(0)
+        quant_c(0)
+        spread_c(nc.scalar.copy, 1, CV, E)
+        product(1, "mid")
+        max1(1)
+        spread_c(nc.vector.tensor_copy, 1, 0, CV)
+        product(2, "old")
+        save_old(2)
+        product(3, "old")
+        save_old(3)
+        turn(4)
+        turn(5)
+        gather(4)
+        product(2, "mid")
+        quant_c(1)
+        max1(2)
+        product(3, "mid")
+        gather(5)
+        max1(3)
+        nc.vector.tensor_copy(out=tau_col[:], in_=tau_raw[:])
+        nc.vector.tensor_copy(out=inv[:], in_=inv_raw[:])
+        for i in range(4):
+            product(i, "new")
+        tb = psum.tile([P, 4, P], F32, name="tb", tag="old")
+        for j in range(4):
+            nc.tensor.transpose(
+                tb[:, j, :], tau_col[:, j : j + 1].to_broadcast([P, P]), ident[:]
+            )
+        part(6)
+        part(7)
+        nc.scalar.copy(out=tau_all[:], in_=tb[:].rearrange("p j q -> p q j"))
+        quant(4)
+        max2(0)
+        quant(5)
+        max2(1)
+        finish(0)
+        max2(2)
+        finish(1)
+        finish(2)
+
+        last = NT - 1
+        for s in range(2, NT // 2):
+            a, b = 2 * s, 2 * s + 1
+            more = b + 2 < NT
+            if more:
+                turn(a + 2)
+                turn(b + 2)
+            max2(a - 1)
+            if a - 2 > 2:
+                finish(a - 2)
+            if more:
+                gather(a + 2)
+            product(a, "old")
+            save_old(a)
+            product(a, "mid")
+            if more:
+                quant(a + 2)
+            finish(a - 1)
+            max1(a)
+            product(a, "new")
+            if more:
+                gather(b + 2)
+                quant(b + 2)
+            if b + 4 < NT:
+                part(a + 4)
+            product(b, "old")
+            save_old(b)
+            if b + 4 < NT:
+                part(b + 4)
+            max2(a)
+            if more:
+                product(b, "mid")
+                max1(b)
+                product(b, "new")
+        finish(last - 1)
+        h0, h1 = (0, 256), (256, E)
+        product(last, "mid", h0)
+        max1(last, h0)
+        product(last, "new", h0)
+        max2(last, h0)
+        product(last, "mid", h1)
+        max1(last, h1)
+        finish(last, h0)
+        product(last, "new", h1, "xt")
+        max2(last, h1)
+        finish(last, h1)

@@ -20,7 +20,7 @@ OP = mybir.AluOpType
 
 DIRECT = 6
 CV = 384
-POOL_F = (0, 1, 2, 3, 12, 13)
+POOL_F = (0, 1, 2, 5, 7, 9, 11, 13, 14)
 
 
 def tile_cosine_prototype_router_s10_kernel(
@@ -74,6 +74,7 @@ def tile_cosine_prototype_router_s10_kernel(
         nc.sync.dma_start(out=a_sb[:], in_=a_words.rearrange("g p b -> p g b"))
         load_z(1, 1)
         nc.sync.dma_start(out=b_sb[:], in_=b_words.rearrange("g p n t -> p g (n t)"))
+        load_scales(nc.sync, b_sc, b_scales)
         load_z(2, 2)
         load_c(0)
         nc.sync.dma_start(out=tau_raw[:], in_=tau.rearrange("(q j) -> q j", j=4))
@@ -84,7 +85,6 @@ def tile_cosine_prototype_router_s10_kernel(
 
         ident = keep.tile([P, P], F32, name="ident")
         make_identity(nc, ident[:])
-        load_scales(nc.gpsimd, b_sc, b_scales)
 
         warm = keep.tile([P, 1], F32, name="warm")
         nc.vector.memset(warm[:], 0.0)
@@ -270,7 +270,9 @@ def tile_cosine_prototype_router_s10_kernel(
         finish(0)
         max2(2)
         finish(1)
+        max2(3)
         finish(2)
+        finish(3)
 
         last = NT - 1
         for s in range(2, NT // 2):
@@ -279,42 +281,35 @@ def tile_cosine_prototype_router_s10_kernel(
             if more:
                 turn(a + 2)
                 turn(b + 2)
-            max2(a - 1)
-            if a - 2 > 2:
-                finish(a - 2)
-            if more:
                 gather(a + 2)
+                quant(a + 2)
             product(a, "old")
             save_old(a)
             product(a, "mid")
-            if more:
-                quant(a + 2)
-            finish(a - 1)
             max1(a)
-            product(a, "new")
+            product(b, "old")
             if more:
                 gather(b + 2)
                 quant(b + 2)
+            save_old(b)
+            product(a, "new")
+            max2(a)
             if b + 4 < NT:
                 part(a + 4)
-            product(b, "old")
-            save_old(b)
-            if b + 4 < NT:
                 part(b + 4)
-            max2(a)
             if more:
                 product(b, "mid")
                 max1(b)
+                finish(a)
                 product(b, "new")
+                max2(b)
+                finish(b)
         finish(last - 1)
         h0, h1 = (0, 256), (256, E)
         product(last, "mid", h0)
-        max1(last, h0)
         product(last, "new", h0)
-        max2(last, h0)
         product(last, "mid", h1)
-        max1(last, h1)
-        finish(last, h0)
         product(last, "new", h1, "xt")
-        max2(last, h1)
-        finish(last, h1)
+        for step in (max1, max2, finish):
+            step(last, h0)
+            step(last, h1)

@@ -20,7 +20,7 @@ OP = mybir.AluOpType
 
 DIRECT = 6
 CV = 384
-POOL_F = (0, 1, 2, 5, 7, 9, 11, 13, 14)
+POOL_F = (0, 1, 2)
 
 
 def tile_cosine_prototype_router_s10_kernel(
@@ -73,18 +73,18 @@ def tile_cosine_prototype_router_s10_kernel(
         load_scales(nc.scalar, a_sc, a_scales)
         nc.sync.dma_start(out=a_sb[:], in_=a_words.rearrange("g p b -> p g b"))
         load_z(1, 1)
-        nc.sync.dma_start(out=b_sb[:], in_=b_words.rearrange("g p n t -> p g (n t)"))
-        load_scales(nc.sync, b_sc, b_scales)
-        load_z(2, 2)
         load_c(0)
-        nc.sync.dma_start(out=tau_raw[:], in_=tau.rearrange("(q j) -> q j", j=4))
-        nc.sync.dma_start(out=inv_raw[:], in_=inv_len.rearrange("(p i) -> p i", i=NT))
+        load_z(2, 2)
         load_c(1)
+        nc.sync.dma_start(out=b_sb[:], in_=b_words.rearrange("g p n t -> p g (n t)"))
         for i in range(4, NT, 2):
             load_z(i, 2)
 
         ident = keep.tile([P, P], F32, name="ident")
         make_identity(nc, ident[:])
+        load_scales(nc.gpsimd, b_sc, b_scales)
+        nc.gpsimd.dma_start(out=tau_raw[:], in_=tau.rearrange("(q j) -> q j", j=4))
+        nc.gpsimd.dma_start(out=inv_raw[:], in_=inv_len.rearrange("(p i) -> p i", i=NT))
 
         warm = keep.tile([P, 1], F32, name="warm")
         nc.vector.memset(warm[:], 0.0)
@@ -196,7 +196,8 @@ def tile_cosine_prototype_router_s10_kernel(
                     out=res[i][:, s], in0=m2[i][:, s], scalar=inv[:, i : i + 1],
                     in1=tau_flat[:, s], op0=OP.mult, op1=OP.mult,
                 )
-            nc.sync.dma_start(out=out_view[:, i, s], in_=res[i][:, s])
+            queue = nc.scalar if i == NT - 1 else nc.sync
+            queue.dma_start(out=out_view[:, i, s], in_=res[i][:, s])
 
         def spread_c(engine_copy, g, lo, hi):
             engine_copy(
@@ -221,52 +222,53 @@ def tile_cosine_prototype_router_s10_kernel(
         quant(1)
         product(0, "old")
         save_old(0)
+        spread_c(nc.vector.tensor_copy, 0, 0, E)
         product(1, "old")
-        spread_c(nc.scalar.copy, 0, CV, E)
-        spread_c(nc.vector.tensor_copy, 0, 0, CV)
-        turn(2)
         save_old(1)
+        quant_c(0)
+        turn(2)
         gather(2)
-        turn(3)
-        product(0, "mid")
         quant(2)
+        turn(3)
         gather(3)
         quant(3)
-        max1(0)
-        quant_c(0)
-        spread_c(nc.scalar.copy, 1, CV, E)
-        product(1, "mid")
-        max1(1)
-        spread_c(nc.vector.tensor_copy, 1, 0, CV)
         product(2, "old")
+        spread_c(nc.scalar.copy, 1, CV, E)
+        spread_c(nc.vector.tensor_copy, 1, 0, CV)
         save_old(2)
         product(3, "old")
         save_old(3)
-        turn(4)
-        turn(5)
-        gather(4)
-        product(2, "mid")
         quant_c(1)
+        product(0, "mid")
+        max1(0)
+        product(1, "mid")
+        max1(1)
+        turn(4)
+        gather(4)
+        turn(5)
+        gather(5)
+        product(2, "mid")
         max1(2)
         product(3, "mid")
-        gather(5)
         max1(3)
         nc.vector.tensor_copy(out=tau_col[:], in_=tau_raw[:])
         nc.vector.tensor_copy(out=inv[:], in_=inv_raw[:])
-        for i in range(4):
-            product(i, "new")
+        quant(4)
+        product(0, "new")
+        product(1, "new")
+        max2(0)
         tb = psum.tile([P, 4, P], F32, name="tb", tag="old")
         for j in range(4):
             nc.tensor.transpose(
                 tb[:, j, :], tau_col[:, j : j + 1].to_broadcast([P, P]), ident[:]
             )
+        nc.scalar.copy(out=tau_all[:], in_=tb[:].rearrange("p j q -> p q j"))
         part(6)
         part(7)
-        nc.scalar.copy(out=tau_all[:], in_=tb[:].rearrange("p j q -> p q j"))
-        quant(4)
-        max2(0)
+        product(2, "new")
         quant(5)
         max2(1)
+        product(3, "new")
         finish(0)
         max2(2)
         finish(1)
@@ -283,6 +285,8 @@ def tile_cosine_prototype_router_s10_kernel(
                 turn(b + 2)
                 gather(a + 2)
                 quant(a + 2)
+            if s > 2:
+                finish(a - 1)
             product(a, "old")
             save_old(a)
             product(a, "mid")
@@ -303,7 +307,6 @@ def tile_cosine_prototype_router_s10_kernel(
                 finish(a)
                 product(b, "new")
                 max2(b)
-                finish(b)
         finish(last - 1)
         h0, h1 = (0, 256), (256, E)
         product(last, "mid", h0)

@@ -20,7 +20,7 @@ OP = mybir.AluOpType
 
 DIRECT = 6
 CV = 384
-POOL_F = (0, 1, 2)
+POOL_F = (0, 1, 2, 5, 7, 9, 11, 13, 14)
 
 
 def tile_cosine_prototype_router_s10_kernel(
@@ -44,7 +44,7 @@ def tile_cosine_prototype_router_s10_kernel(
         c_grp = [keep.tile([P, E, 4], BF16, name=f"c_grp{g}", align_bytes=64) for g in range(G)]
         c_codes = keep.tile([P, G, E], U32, name="c_codes", align_bytes=64)
         c_sc = keep.tile([P, G, E], U8, name="c_sc", align_bytes=64)
-        tau_raw = keep.tile([P, 4], BF16, name="tau_raw")
+        tau_all = keep.tile([P, E], BF16, name="tau_all")
         inv_raw = keep.tile([P, NT], BF16, name="inv_raw")
         rows = {}
 
@@ -73,25 +73,25 @@ def tile_cosine_prototype_router_s10_kernel(
         load_scales(nc.scalar, a_sc, a_scales)
         nc.sync.dma_start(out=a_sb[:], in_=a_words.rearrange("g p b -> p g b"))
         load_z(1, 1)
+        load_z(2, 1)
         load_c(0)
-        load_z(2, 2)
+        load_z(3, 1)
         load_c(1)
         nc.sync.dma_start(out=b_sb[:], in_=b_words.rearrange("g p n t -> p g (n t)"))
+        load_scales(nc.sync, b_sc, b_scales)
         for i in range(4, NT, 2):
             load_z(i, 2)
+            if i == 8:
+                nc.sync.dma_start(out=tau_all[:], in_=tau.partition_broadcast(P))
 
         ident = keep.tile([P, P], F32, name="ident")
         make_identity(nc, ident[:])
-        load_scales(nc.gpsimd, b_sc, b_scales)
-        nc.gpsimd.dma_start(out=tau_raw[:], in_=tau.rearrange("(q j) -> q j", j=4))
         nc.gpsimd.dma_start(out=inv_raw[:], in_=inv_len.rearrange("(p i) -> p i", i=NT))
 
         warm = keep.tile([P, 1], F32, name="warm")
         nc.vector.memset(warm[:], 0.0)
         nc.scalar.copy(out=warm[:], in_=warm[:])
 
-        tau_col = keep.tile([P, 4], F32, name="tau_col")
-        tau_all = keep.tile([P, P, 4], F32, name="tau_all")
         inv = keep.tile([P, NT], F32, name="inv")
 
         apart, bank, grouped, codes, scales = {}, {}, {}, {}, {}
@@ -177,24 +177,27 @@ def tile_cosine_prototype_router_s10_kernel(
                 out=m2[i][:, s], in0=new[i, cols[0]][:], in1=m1[i][:, s], op=OP.max
             )
 
-        tau_flat = tau_all[:].rearrange("p q j -> p (q j)")
+        factor = {}
+
+        def weigh(i):
+            factor[i] = work.tile([P, E], F32, name="factor")
+            nc.scalar.activation(
+                out=factor[i][:], in_=tau_all[:], func=mybir.ActivationFunctionType.Copy,
+                scale=inv[:, i : i + 1],
+            )
 
         def finish(i, cols=(0, E)):
             if i not in res:
                 res[i] = work.tile([P, E], F32, name="res")
             s = slice(cols[0], cols[1])
             if i in POOL_F:
-                nc.gpsimd.tensor_scalar(
-                    out=m2[i][:, s], in0=m2[i][:, s], scalar1=inv[:, i : i + 1], scalar2=0.0,
-                    op0=OP.mult, op1=OP.add,
-                )
                 nc.gpsimd.tensor_tensor(
-                    out=res[i][:, s], in0=m2[i][:, s], in1=tau_flat[:, s], op=OP.mult
+                    out=res[i][:, s], in0=m2[i][:, s], in1=factor[i][:, s], op=OP.mult
                 )
             else:
                 nc.vector.scalar_tensor_tensor(
                     out=res[i][:, s], in0=m2[i][:, s], scalar=inv[:, i : i + 1],
-                    in1=tau_flat[:, s], op0=OP.mult, op1=OP.mult,
+                    in1=tau_all[:, s], op0=OP.mult, op1=OP.mult,
                 )
             queue = nc.scalar if i == NT - 1 else nc.sync
             queue.dma_start(out=out_view[:, i, s], in_=res[i][:, s])
@@ -220,28 +223,28 @@ def tile_cosine_prototype_router_s10_kernel(
         turn(1)
         gather(1)
         quant(1)
+        turn(2)
+        gather(2)
         product(0, "old")
         save_old(0)
+        quant(2)
         spread_c(nc.vector.tensor_copy, 0, 0, E)
         product(1, "old")
         save_old(1)
-        quant_c(0)
-        turn(2)
-        gather(2)
-        quant(2)
         turn(3)
         gather(3)
         quant(3)
+        quant_c(0)
         product(2, "old")
-        spread_c(nc.scalar.copy, 1, CV, E)
-        spread_c(nc.vector.tensor_copy, 1, 0, CV)
         save_old(2)
+        spread_c(nc.vector.tensor_copy, 1, 0, CV)
+        spread_c(nc.scalar.copy, 1, CV, E)
+        product(0, "mid")
         product(3, "old")
         save_old(3)
-        quant_c(1)
-        product(0, "mid")
-        max1(0)
         product(1, "mid")
+        max1(0)
+        quant_c(1)
         max1(1)
         turn(4)
         gather(4)
@@ -251,29 +254,25 @@ def tile_cosine_prototype_router_s10_kernel(
         max1(2)
         product(3, "mid")
         max1(3)
-        nc.vector.tensor_copy(out=tau_col[:], in_=tau_raw[:])
         nc.vector.tensor_copy(out=inv[:], in_=inv_raw[:])
-        quant(4)
         product(0, "new")
-        product(1, "new")
         max2(0)
-        tb = psum.tile([P, 4, P], F32, name="tb", tag="old")
-        for j in range(4):
-            nc.tensor.transpose(
-                tb[:, j, :], tau_col[:, j : j + 1].to_broadcast([P, P]), ident[:]
-            )
-        nc.scalar.copy(out=tau_all[:], in_=tb[:].rearrange("p j q -> p q j"))
+        quant(4)
+        product(1, "new")
+        max2(1)
         part(6)
         part(7)
-        product(2, "new")
+        weigh(0)
+        weigh(1)
+        weigh(2)
+        product(2, "new", tag="mid")
         quant(5)
-        max2(1)
-        product(3, "new")
-        finish(0)
         max2(2)
+        product(3, "new", tag="mid")
+        finish(0)
         finish(1)
-        max2(3)
         finish(2)
+        max2(3)
         finish(3)
 
         last = NT - 1
@@ -301,6 +300,9 @@ def tile_cosine_prototype_router_s10_kernel(
             if b + 4 < NT:
                 part(a + 4)
                 part(b + 4)
+            for i in (a, b):
+                if i in POOL_F:
+                    weigh(i)
             if more:
                 product(b, "mid")
                 max1(b)

from contextlib import ExitStack

import concourse.mybir as mybir
from concourse.masks import make_identity

T, D, E = 2048, 1024, 512
P = 128
NT = T // P
G = 2
FLOPS = 3 * 2 * T * D * E

F32 = mybir.dt.float32
BF16 = mybir.dt.bfloat16
I32 = mybir.dt.int32
U32 = mybir.dt.uint32
U8 = mybir.dt.uint8
FP8X4 = mybir.dt.float8_e4m3fn_x4
FP4X4 = mybir.dt.float4_e2m1fn_x4
OP = mybir.AluOpType

DIRECT = 6
CV = 384
POOL_F = (0, 1, 2, 5, 7, 9, 11, 13, 14)


def tile_cosine_prototype_router_s10_kernel(
    tc, z, a_words, a_scales, b_words, b_scales, c, inv_len, tau, out
):
    nc = tc.nc
    z_view = z.rearrange("(p i) d -> p i d", i=NT)
    out_view = out.rearrange("(p i) e -> p i e", i=NT)

    with ExitStack() as ctx:
        keep = ctx.enter_context(tc.tile_pool(name="keep", bufs=1))
        work = ctx.enter_context(tc.tile_pool(name="work", bufs=6))
        psum = ctx.enter_context(tc.psum_pool(name="psum", bufs=2))
        ctx.enter_context(tc.manual_schedule())

        a_sb = keep.tile([P, G, 2 * E], U8, name="a_sb", align_bytes=64)
        b_sb = keep.tile([P, G, 4 * E], U8, name="b_sb", align_bytes=64)
        a_sc = keep.tile([P, G, E], U8, name="a_sc", align_bytes=64)
        b_sc = keep.tile([P, G, E], U8, name="b_sc", align_bytes=64)
        c_raw = [keep.tile([P, 4, E], BF16, name=f"c_raw{g}") for g in range(G)]
        c_grp = [keep.tile([P, E, 4], BF16, name=f"c_grp{g}", align_bytes=64) for g in range(G)]
        c_codes = keep.tile([P, G, E], U32, name="c_codes", align_bytes=64)
        c_sc = keep.tile([P, G, E], U8, name="c_sc", align_bytes=64)
        tau_all = keep.tile([P, E], BF16, name="tau_all")
        inv_raw = keep.tile([P, NT], BF16, name="inv_raw")
        rows = {}

        def load_z(i, n):
            zt = keep.tile([P, n, D], BF16, name=f"z{i}", align_bytes=64)
            nc.sync.dma_start(out=zt[:], in_=z_view[:, i : i + n, :])
            for k in range(n):
                rows[i + k] = zt[:, k, :].bitcast(F32)

        def load_c(g):
            nc.sync.dma_start(
                out=c_raw[g][:],
                in_=c[512 * g : 512 * (g + 1), :].rearrange("(p j) e -> p j e", j=4),
            )

        def load_scales(queue, tile, src):
            for q in range(4):
                queue.dma_start(
                    out=tile[32 * q : 32 * q + 4].bitcast(I32),
                    in_=src[:, 4 * q : 4 * q + 4, :].rearrange("g r n -> r g n").bitcast(I32),
                )

        load_z(0, 1)
        nc.vector.memset(a_sc[:].bitcast(I32), 0)
        nc.vector.memset(b_sc[:].bitcast(I32), 0)
        load_scales(nc.scalar, a_sc, a_scales)
        nc.sync.dma_start(out=a_sb[:], in_=a_words.rearrange("g p b -> p g b"))
        load_z(1, 1)
        load_z(2, 1)
        load_c(0)
        load_z(3, 1)
        load_c(1)
        nc.sync.dma_start(out=b_sb[:], in_=b_words.rearrange("g p n t -> p g (n t)"))
        load_scales(nc.sync, b_sc, b_scales)
        for i in range(4, NT, 2):
            load_z(i, 2)
            if i == 8:
                nc.sync.dma_start(out=tau_all[:], in_=tau.partition_broadcast(P))

        ident = keep.tile([P, P], F32, name="ident")
        make_identity(nc, ident[:])
        nc.gpsimd.dma_start(out=inv_raw[:], in_=inv_len.rearrange("(p i) -> p i", i=NT))

        warm = keep.tile([P, 1], F32, name="warm")
        nc.vector.memset(warm[:], 0.0)
        nc.scalar.copy(out=warm[:], in_=warm[:])

        inv = keep.tile([P, NT], F32, name="inv")

        apart, bank, grouped, codes, scales = {}, {}, {}, {}, {}
        old, mid, new, s_old, m1, m2, res = {}, {}, {}, {}, {}, {}, {}

        def part(i):
            apart[i] = work.tile([P, G, 2, P], F32, name="apart")
            nc.scalar.copy(
                out=apart[i][:], in_=rows[i].rearrange("p (g w u) -> p g u w", g=G, u=2)
            )

        def turn(i, halves=(0, 1), tag="xt"):
            b = psum.tile([P, len(halves), 2, P], F32, name="xt", tag=tag)
            for n, g in enumerate(halves):
                for u in range(2):
                    if i < DIRECT:
                        src = rows[i][:, 256 * g + u : 256 * (g + 1) : 2]
                    else:
                        src = apart[i][:, g, u, :]
                    nc.tensor.transpose(b[:, n, u, :], src, ident[:])
                bank[i, g] = b[:, n]
            bank[i] = b

        def gather(i, halves=(0, 1)):
            if i not in grouped:
                grouped[i] = work.tile([P, G, P, 4], BF16, name="grouped", align_bytes=64)
            lo, hi = halves[0], halves[-1] + 1
            dst = grouped[i][:, lo:hi].rearrange("p g r t -> p (g r t)").bitcast(F32)
            nc.scalar.copy(
                out=dst.rearrange("p (g r u) -> p g r u", r=P, u=2),
                in_=bank[i][:].rearrange("p g u r -> p g r u"),
            )

        def quant(i, halves=(0, 1)):
            if i not in codes:
                codes[i] = work.tile([P, G, P], U32, name="codes", align_bytes=64)
                scales[i] = work.tile([P, G, P], U8, name="scales", align_bytes=64)
            lo, hi = halves[0], halves[-1] + 1
            nc.vector.quantize_mx(
                out=codes[i][:, lo:hi].rearrange("p g r -> p (g r)").bitcast(FP8X4),
                scales=scales[i][:, lo:hi].rearrange("p g r -> p (g r)"),
                in_=grouped[i][:, lo:hi].rearrange("p g r t -> p (g r t)"),
            )

        def product(i, which, cols=(0, E), tag=None):
            n0, n1 = cols
            b = psum.tile([P, n1 - n0], F32, name=which, tag=tag or which)
            for g in range(G):
                if which == "old":
                    rhs, sc = a_sb[:, g, 2 * n0 : 2 * n1].bitcast(FP4X4), a_sc[:, g, n0:n1]
                elif which == "mid":
                    rhs, sc = b_sb[:, g, 4 * n0 : 4 * n1].bitcast(FP8X4), b_sc[:, g, n0:n1]
                else:
                    rhs, sc = c_codes[:, g, n0:n1].bitcast(FP8X4), c_sc[:, g, n0:n1]
                nc.tensor.matmul_mx(
                    out=b[:],
                    lhsT=codes[i][:, g, :].bitcast(FP8X4),
                    lhsT_scale=scales[i][:, g, :],
                    rhs=rhs,
                    rhs_scale=sc,
                    start=(g == 0),
                    stop=(g == G - 1),
                )
            {"old": old, "mid": mid, "new": new}[which][i, n0] = b

        def save_old(i):
            s_old[i] = work.tile([P, E], F32, name="s_old")
            nc.scalar.copy(out=s_old[i][:], in_=old[i, 0][:])

        def max1(i, cols=(0, E)):
            if i not in m1:
                m1[i] = work.tile([P, E], F32, name="m1")
            s = slice(cols[0], cols[1])
            nc.vector.tensor_tensor(
                out=m1[i][:, s], in0=mid[i, cols[0]][:], in1=s_old[i][:, s], op=OP.max
            )

        def max2(i, cols=(0, E)):
            if i not in m2:
                m2[i] = work.tile([P, E], F32, name="m2")
            s = slice(cols[0], cols[1])
            nc.vector.tensor_tensor(
                out=m2[i][:, s], in0=new[i, cols[0]][:], in1=m1[i][:, s], op=OP.max
            )

        factor = {}

        def weigh(i):
            factor[i] = work.tile([P, E], F32, name="factor")
            nc.scalar.activation(
                out=factor[i][:], in_=tau_all[:], func=mybir.ActivationFunctionType.Copy,
                scale=inv[:, i : i + 1],
            )

        def finish(i, cols=(0, E)):
            if i not in res:
                res[i] = work.tile([P, E], F32, name="res")
            s = slice(cols[0], cols[1])
            if i in POOL_F:
                nc.gpsimd.tensor_tensor(
                    out=res[i][:, s], in0=m2[i][:, s], in1=factor[i][:, s], op=OP.mult
                )
            else:
                nc.vector.scalar_tensor_tensor(
                    out=res[i][:, s], in0=m2[i][:, s], scalar=inv[:, i : i + 1],
                    in1=tau_all[:, s], op0=OP.mult, op1=OP.mult,
                )
            queue = nc.scalar if i == NT - 1 else nc.sync
            queue.dma_start(out=out_view[:, i, s], in_=res[i][:, s])

        def spread_c(engine_copy, g, lo, hi):
            engine_copy(
                out=c_grp[g][:, lo:hi, :], in_=c_raw[g][:, :, lo:hi].rearrange("p j e -> p e j")
            )

        def quant_c(g):
            nc.vector.quantize_mx(
                out=c_codes[:, g, :].bitcast(FP8X4),
                scales=c_sc[:, g, :],
                in_=c_grp[g][:].rearrange("p e j -> p (e j)"),
            )

        turn(0, (0,), "xt")
        gather(0, (0,))
        quant(0, (0,))
        turn(0, (1,), "new")
        gather(0, (1,))
        quant(0, (1,))
        turn(1)
        gather(1)
        quant(1)
        turn(2)
        gather(2)
        product(0, "old")
        save_old(0)
        quant(2)
        spread_c(nc.vector.tensor_copy, 0, 0, E)
        product(1, "old")
        save_old(1)
        turn(3)
        gather(3)
        quant(3)
        quant_c(0)
        product(2, "old")
        save_old(2)
        spread_c(nc.vector.tensor_copy, 1, 0, CV)
        spread_c(nc.scalar.copy, 1, CV, E)
        product(0, "mid")
        product(3, "old")
        save_old(3)
        product(1, "mid")
        max1(0)
        quant_c(1)
        max1(1)
        turn(4)
        gather(4)
        turn(5)
        gather(5)
        product(2, "mid")
        max1(2)
        product(3, "mid")
        max1(3)
        nc.vector.tensor_copy(out=inv[:], in_=inv_raw[:])
        product(0, "new")
        max2(0)
        quant(4)
        product(1, "new")
        max2(1)
        part(6)
        part(7)
        weigh(0)
        weigh(1)
        weigh(2)
        product(2, "new", tag="mid")
        quant(5)
        max2(2)
        product(3, "new", tag="mid")
        finish(0)
        finish(1)
        finish(2)
        max2(3)
        finish(3)

        last = NT - 1
        for s in range(2, NT // 2):
            a, b = 2 * s, 2 * s + 1
            more = b + 2 < NT
            if more:
                turn(a + 2)
                turn(b + 2)
                gather(a + 2)
                quant(a + 2)
            if s > 2:
                finish(a - 1)
            product(a, "old")
            save_old(a)
            product(a, "mid")
            max1(a)
            product(b, "old")
            if more:
                gather(b + 2)
                quant(b + 2)
            save_old(b)
            product(a, "new")
            max2(a)
            if b + 4 < NT:
                part(a + 4)
                part(b + 4)
            for i in (a, b):
                if i in POOL_F:
                    weigh(i)
            if more:
                product(b, "mid")
                max1(b)
                finish(a)
                product(b, "new")
                max2(b)
        finish(last - 1)
        h0, h1 = (0, 256), (256, E)
        product(last, "mid", h0)
        product(last, "new", h0)
        product(last, "mid", h1)
        product(last, "new", h1, "xt")
        for step in (max1, max2, finish):
            step(last, h0)
            step(last, h1)
